import numpy as np
import ml_dtypes


def mxq(x, axis, fmt="e4m3"):
    dtype, down = {"e4m3": (ml_dtypes.float8_e4m3fn, 7), "e5m2": (ml_dtypes.float8_e5m2, 14)}[fmt]
    v = np.moveaxis(np.asarray(x, np.float32).astype(ml_dtypes.bfloat16).astype(np.float64), axis, -1)
    blocks = v.reshape(v.shape[:-1] + (-1, 32))
    amax = np.abs(blocks).max(-1, keepdims=True)
    byte = np.maximum(np.where(amax > 0, np.frexp(amax)[1] - 1 + 127, 0) - down, 1)
    scale = np.exp2(byte - 127.0)
    codes = (blocks / scale).astype(np.float32).astype(dtype).astype(np.float64)
    return np.moveaxis((codes * scale).reshape(v.shape), -1, axis)


WIDE = False


def mx_kscale(k):
    if not WIDE:
        return np.ones(k)
    levels = np.array([10, -10, 5, -5, 0])
    if k % 512:
        return np.exp2(np.random.permutation(np.resize(levels, k // 32))).repeat(32)
    a = np.empty((k // 512, 16))
    for p in range(k // 512):
        a[p, :8] = np.random.permutation(np.resize(levels, 8))
        for g in range(8):
            far = levels[np.abs(levels - a[p, g]) >= 10]
            a[p, g + 8] = far[np.random.randint(len(far))]
    return np.exp2(a.ravel()).repeat(32)


def f64(x):
    return np.asarray(x).astype(np.float64)


def striped(idx):
    return np.tile(idx.reshape(-1, 16).T, (8, 1)).astype(np.uint16)


def unstriped(offs):
    return offs[:16].T.reshape(-1).astype(np.int64)


def pack_weight(w):
    k, n = w.shape
    w = f64(np.asarray(w, np.float32).astype(ml_dtypes.bfloat16)).reshape(k // 32, 32, n)
    amax = np.abs(w).max(1)
    byte = np.clip(np.where(amax > 0, np.frexp(amax)[1] - 1 + 127 - 7, 1), 1, 254)
    scaled = (w * np.exp2(127.0 - byte)[:, None, :]).reshape(k, n).astype(np.float32)
    words = np.ascontiguousarray(scaled.reshape(k // 512, 128, 4, n).transpose(0, 1, 3, 2)).astype(ml_dtypes.float8_e4m3fn).view(np.uint8)
    return words, np.ascontiguousarray(byte.astype(np.uint8).reshape(k // 512, 16, n))


def unpack_weight(words, scales):
    g, p, n, _ = words.shape
    vals = np.ascontiguousarray(words).view(ml_dtypes.float8_e4m3fn).astype(np.float64) * np.repeat(np.exp2(scales.astype(np.float64) - 127.0), 8, axis=1)[..., None]
    return vals.transpose(0, 1, 3, 2).reshape(g * 512, n)


def planes(y):
    n, m = y.shape
    v = y.astype(np.float32).astype(ml_dtypes.bfloat16).astype(np.float64).reshape(n // 32, 32, m)
    top = np.abs(v).max(1)
    byte = np.clip(np.where(top > 0, np.frexp(top)[1] - 1 + 127 - 7, 1), 1, 254)
    codes = (v * np.exp2(127.0 - byte)[:, None, :]).reshape(n, m).astype(np.float32).astype(ml_dtypes.float8_e4m3fn).view(np.uint8)
    words = codes.reshape(n // 512, 128, 4, m).transpose(0, 1, 3, 2)
    return np.ascontiguousarray(words), np.ascontiguousarray(byte.astype(np.uint8).reshape(n // 512, 16, m))


def relu(v):
    return np.maximum(v, 0.0)


K, T, S, V, H, N = 1024, 1024, 512, 256, 512, 512


def setup_inputs():
    n = np.random.standard_normal
    s = mx_kscale(K)[:, None]
    u = mx_kscale(H)
    near = np.random.permutation(S)
    packed_xT = pack_weight(n((K, T)) * s)
    return {
        "x_words": packed_xT[0],
        "x_scales": packed_xT[1],
        "w1": (n((K, H)) / np.sqrt(2 * K) / s * u).astype(np.float32),
        "w2": (n((K, H)) / np.sqrt(2 * K) / s * u).astype(np.float32),
        "w3": (n((H, N)) / np.sqrt(2 * H) / u[:, None]).astype(np.float32),
        "w4": (n((H, N)) / np.sqrt(2 * H) / u[:, None]).astype(np.float32),
        "offs": striped(np.random.permutation(T)[:S]),
        "right": striped(np.random.permutation(T)[:S]),
        "up1": striped(near[:V]),
        "up2": striped(near[V:]),
    }


def reference(x_words, x_scales, w1, w2, w3, w4, offs, right, up1, up2):
    xq = unpack_weight(x_words, x_scales)[:, unstriped(offs)]
    x_right = unpack_weight(x_words, x_scales)[:, unstriped(right)]
    h = relu(mxq(f64(w1), 0, "e4m3").T @ xq + mxq(f64(w2), 0, "e4m3").T @ x_right)
    a = h[:, unstriped(up1)]
    ee = h[:, unstriped(up2)]
    out_0 = relu(mxq(f64(w3), 0, "e4m3").T @ mxq(a, 0, "e4m3") + mxq(f64(w4), 0, "e4m3").T @ mxq(ee, 0, "e4m3"))
    return (out_0,) + planes(out_0)

@@ -1,0 +1,218 @@
+from contextlib import ExitStack
+
+import concourse.mybir as mybir
+
+K, T, S, V, H, N = 1024, 1024, 512, 256, 512, 512
+FLOPS = 2 * (2 * K * H * S + 2 * H * N * V)
+
+F32 = mybir.dt.float32
+BF16 = mybir.dt.bfloat16
+I32 = mybir.dt.int32
+U32 = mybir.dt.uint32
+U16 = mybir.dt.uint16
+U8 = mybir.dt.uint8
+FP8X4 = mybir.dt.float8_e4m3fn_x4
+RELU = mybir.ActivationFunctionType.Relu
+
+P = 128
+PACK = 4
+K_PASS = P * PACK
+
+
+def tile_picked_yrecnn_relu_po_kernel(
+    tc, x_words, x_scales, w1, w2, w3, w4, offs, right, up1, up2, out_0, out_1, out_2
+):
+    nc = tc.nc
+    with ExitStack() as ctx:
+        keep = ctx.enter_context(tc.tile_pool(name="keep", bufs=1))
+        psum = ctx.enter_context(tc.psum_pool(name="psum", bufs=1))
+
+        weights = {
+            "w1p0": w1[0:K_PASS, :], "w1p1": w1[K_PASS:K, :],
+            "w2p0": w2[0:K_PASS, :], "w2p1": w2[K_PASS:K, :],
+            "w3": w3, "w4": w4,
+        }
+        raw, rounded, codes, scales = {}, {}, {}, {}
+        for name in weights:
+            raw[name] = keep.tile([P, PACK, K_PASS], F32, name=f"raw_{name}")
+            for pair in range(2):
+                rounded[name, pair] = keep.tile([P, 2, P, PACK], BF16, name=f"rounded_{name}_{pair}", align_bytes=64)
+            codes[name] = keep.tile([P, K_PASS], U32, name=f"codes_{name}", align_bytes=64)
+            scales[name] = keep.tile([P, K_PASS], U8, name=f"scales_{name}", align_bytes=64)
+
+        def load_weight(name):
+            nc.sync.dma_start(out=raw[name][:], in_=weights[name].rearrange("(p j) c -> p j c", j=PACK))
+
+        def load_list(source, name):
+            tile = keep.tile(list(source.shape), U16, name=name)
+            nc.sync.dma_start(out=tile[:], in_=source)
+            return tile
+
+        def round_weight(copy, name, pair):
+            src = raw[name][:].rearrange("p j (m u e) -> p u m j e", u=2, e=2)[:, pair]
+            dst = rounded[name, pair][:].rearrange("p e m j -> p m j e")
+            copy(out=dst, in_=src)
+
+        def quantize_weight(name, pair, pieces=1):
+            flat = rounded[name, pair][:].rearrange("p e m j -> p (e m j)")
+            width = 2 * P // pieces
+            for piece in range(pieces):
+                cols = slice(pair * 2 * P + piece * width, pair * 2 * P + (piece + 1) * width)
+                nc.vector.quantize_mx(
+                    out=codes[name][:, cols].bitcast(FP8X4),
+                    scales=scales[name][:, cols],
+                    in_=flat[:, piece * width * PACK : (piece + 1) * width * PACK],
+                )
+
+        table_words = [keep.tile([P, T], I32, name=f"table_words{o}") for o in range(2)]
+        table_scales = keep.tile([P, T], U8, name="table_scales")
+
+        def load_words(o):
+            nc.sync.dma_start(out=table_words[o][:], in_=x_words[o].rearrange("p c r -> p (c r)").bitcast(I32))
+
+        warm = keep.tile([P, 8], F32, name="warm")
+        warm_out = keep.tile([P, 8], F32, name="warm_out")
+        nc.vector.memset(table_scales[:].bitcast(I32), 0)
+        nc.vector.memset(warm[:], 0.0)
+        nc.scalar.activation(out=warm_out[:], in_=warm[:], func=RELU)
+
+        load_weight("w1p0")
+        for q in range(4):
+            nc.sync.dma_start(
+                out=table_scales[32 * q : 32 * q + 8, :].bitcast(I32),
+                in_=x_scales[:, 4 * q : 4 * q + 4, :].bitcast(I32),
+            )
+        left_list = load_list(offs, "left_list")
+        right_list = load_list(right, "right_list")
+        load_words(0)
+        load_weight("w2p0")
+        load_words(1)
+        load_weight("w1p1")
+        load_weight("w2p1")
+        up1_list = load_list(up1, "up1_list")
+        up2_list = load_list(up2, "up2_list")
+        load_weight("w3")
+        load_weight("w4")
+
+        picked_words, picked_scales = {}, {}
+
+        def gather_words(side, picks, o):
+            picked_words[side, o] = keep.tile([P, S], U32, name=f"picked_words_{side}{o}", align_bytes=64)
+            nc.vector.tensor_copy(out=picked_words[side, o][:], in_=table_words[o][:].bitcast(U32).indirect(picks[:]))
+
+        def gather_scales(side, picks):
+            picked_scales[side] = keep.tile([P, S], U8, name=f"picked_scales_{side}", align_bytes=64)
+            nc.vector.tensor_copy(out=picked_scales[side][:], in_=table_scales[:].indirect(picks[:]))
+
+        h_banks = [psum.tile([P, S], F32, name=f"h_bank{t}") for t in range(PACK)]
+        y_banks = [psum.tile([P, V], F32, name=f"y_bank{t}") for t in range(PACK)]
+
+        def product(bank, name, t, words, plane, start, stop):
+            cols = slice(t * P, (t + 1) * P)
+            nc.tensor.matmul_mx(
+                out=bank[:],
+                lhsT=codes[name][:, cols].bitcast(FP8X4),
+                lhsT_scale=scales[name][:, cols],
+                rhs=words.bitcast(FP8X4),
+                rhs_scale=plane,
+                start=start,
+                stop=stop,
+            )
+
+        def first_products(name, side, o, start, stop):
+            for t in range(PACK):
+                product(h_banks[t], name, t, picked_words[side, o][:], picked_scales[side][4 * o : P, :], start, stop)
+
+        def round_pass(name):
+            for pair in range(2):
+                round_weight(nc.scalar.copy, name, pair)
+
+        round_pass("w1p0")
+        gather_scales("left", left_list)
+        gather_scales("right", right_list)
+        gather_words("left", left_list, 0)
+        gather_words("right", right_list, 0)
+        quantize_weight("w1p0", 0)
+        quantize_weight("w1p0", 1)
+        first_products("w1p0", "left", 0, True, False)
+
+        round_pass("w2p0")
+        gather_words("left", left_list, 1)
+        gather_words("right", right_list, 1)
+        quantize_weight("w2p0", 0)
+        quantize_weight("w2p0", 1)
+        first_products("w2p0", "right", 0, False, False)
+
+        round_weight(nc.scalar.copy, "w1p1", 0)
+        round_weight(nc.vector.tensor_copy, "w1p1", 1)
+        quantize_weight("w1p1", 0)
+        quantize_weight("w1p1", 1)
+        first_products("w1p1", "left", 1, False, False)
+
+        round_weight(nc.vector.tensor_copy, "w2p1", 0)
+        round_weight(nc.scalar.copy, "w2p1", 1)
+        quantize_weight("w2p1", 0, 2)
+        quantize_weight("w2p1", 1, 2)
+        first_products("w2p1", "right", 1, False, True)
+
+        hidden = [keep.tile([P, S], F32, name=f"hidden{t}") for t in range(PACK)]
+        nc.vector.tensor_scalar_max(hidden[0][:], h_banks[0][:], 0.0)
+        for t in range(1, PACK):
+            nc.scalar.activation(out=hidden[t][:], in_=h_banks[t][:], func=RELU)
+
+        children, child_rounded, child_codes, child_scales = {}, {}, {}, {}
+        for side in ("a", "ee"):
+            children[side] = keep.tile([P, PACK, V], F32, name=f"children_{side}")
+            child_rounded[side] = keep.tile([P, V, PACK], BF16, name=f"child_rounded_{side}", align_bytes=64)
+            child_codes[side] = keep.tile([P, V], U32, name=f"child_codes_{side}", align_bytes=64)
+            child_scales[side] = keep.tile([P, V], U8, name=f"child_scales_{side}", align_bytes=64)
+
+        def interleave(copy, dst, src):
+            copy(
+                out=dst[:].rearrange("p (c i) t -> p c t i", i=4),
+                in_=src[:].rearrange("p t (c i) -> p c t i", i=4),
+            )
+
+        def quantize_tile(words, plane, values):
+            nc.vector.quantize_mx(
+                out=words[:].bitcast(FP8X4), scales=plane[:], in_=values[:].rearrange("p v t -> p (v t)")
+            )
+
+        for t in range(PACK):
+            nc.vector.tensor_copy(out=children["a"][:, t, :], in_=hidden[t][:].indirect(up1_list[:]))
+            nc.vector.tensor_copy(out=children["ee"][:, t, :], in_=hidden[t][:].indirect(up2_list[:]))
+        round_pass("w3")
+        round_pass("w4")
+        interleave(nc.vector.tensor_copy, child_rounded["a"], children["a"])
+        interleave(nc.vector.tensor_copy, child_rounded["ee"], children["ee"])
+        quantize_weight("w3", 0)
+        quantize_weight("w3", 1)
+        quantize_tile(child_codes["a"], child_scales["a"], child_rounded["a"])
+        for t in range(PACK):
+            product(y_banks[t], "w3", t, child_codes["a"][:], child_scales["a"][:], True, False)
+        quantize_tile(child_codes["ee"], child_scales["ee"], child_rounded["ee"])
+        quantize_weight("w4", 0)
+        quantize_weight("w4", 1)
+        for t in range(PACK):
+            product(y_banks[t], "w4", t, child_codes["ee"][:], child_scales["ee"][:], False, True)
+
+        y = keep.tile([P, PACK, V], F32, name="y")
+        y_rounded = keep.tile([P, V, PACK], BF16, name="y_rounded", align_bytes=64)
+        y_codes = keep.tile([P, V], I32, name="y_codes", align_bytes=64)
+        y_scales = keep.tile([P, V], U8, name="y_scales", align_bytes=64)
+        y_rows = out_0.rearrange("(p t) v -> p t v", t=PACK)
+        for t in range(PACK):
+            if t % 2 == 0:
+                nc.scalar.activation(out=y[:, t, :], in_=y_banks[t][:], func=RELU)
+            else:
+                nc.vector.tensor_scalar_max(y[:, t, :], y_banks[t][:], 0.0)
+                nc.sync.dma_start(out=y_rows[:, t - 1 : t + 1, :], in_=y[:, t - 1 : t + 1, :])
+        interleave(nc.vector.tensor_copy, y_rounded, y)
+        quantize_tile(y_codes, y_scales, y_rounded)
+        nc.sync.dma_start(out=out_1[0].rearrange("p c r -> p (c r)").bitcast(I32), in_=y_codes[:])
+        for q in range(4):
+            queue = nc.scalar if q % 2 == 0 else nc.sync
+            queue.dma_start(
+                out=out_2[0, 4 * q : 4 * q + 4, :].bitcast(I32),
+                in_=y_scales[32 * q : 32 * q + 4, :].bitcast(I32),
+            )

@@ -17,6 +17,7 @@ RELU = mybir.ActivationFunctionType.Relu
 P = 128
 PACK = 4
 K_PASS = P * PACK
+WARM_PASSES = 4
 
 
 def tile_picked_yrecnn_relu_po_kernel(
@@ -34,7 +35,7 @@ def tile_picked_yrecnn_relu_po_kernel(
         }
         raw, rounded, codes, scales = {}, {}, {}, {}
         for name in weights:
-            raw[name] = keep.tile([P, PACK, K_PASS], F32, name=f"raw_{name}")
+            raw[name] = keep.tile([P, PACK, K_PASS], F32, name=f"raw_{name}", align_bytes=64)
             for pair in range(2):
                 rounded[name, pair] = keep.tile([P, 2, P, PACK], BF16, name=f"rounded_{name}_{pair}", align_bytes=64)
             codes[name] = keep.tile([P, K_PASS], U32, name=f"codes_{name}", align_bytes=64)
@@ -48,9 +49,9 @@ def tile_picked_yrecnn_relu_po_kernel(
             nc.sync.dma_start(out=tile[:], in_=source)
             return tile
 
-        def round_weight(copy, name, pair):
-            src = raw[name][:].rearrange("p j (m u e) -> p u m j e", u=2, e=2)[:, pair]
-            dst = rounded[name, pair][:].rearrange("p e m j -> p m j e")
+        def round_weight(copy, name, pair, start=0, stop=P):
+            src = raw[name][:].rearrange("p j (m u e) -> p u m j e", u=2, e=2)[:, pair, start:stop]
+            dst = rounded[name, pair][:, :, start:stop, :].rearrange("p e m j -> p m j e")
             copy(out=dst, in_=src)
 
         def quantize_weight(name, pair, pieces=1):
@@ -76,15 +77,15 @@ def tile_picked_yrecnn_relu_po_kernel(
         nc.vector.memset(warm[:], 0.0)
         nc.scalar.activation(out=warm_out[:], in_=warm[:], func=RELU)
 
-        load_weight("w1p0")
+        load_words(0)
+        left_list = load_list(offs, "left_list")
+        right_list = load_list(right, "right_list")
         for q in range(4):
             nc.sync.dma_start(
                 out=table_scales[32 * q : 32 * q + 8, :].bitcast(I32),
                 in_=x_scales[:, 4 * q : 4 * q + 4, :].bitcast(I32),
             )
-        left_list = load_list(offs, "left_list")
-        right_list = load_list(right, "right_list")
-        load_words(0)
+        load_weight("w1p0")
         load_weight("w2p0")
         load_words(1)
         load_weight("w1p1")
@@ -128,23 +129,24 @@ def tile_picked_yrecnn_relu_po_kernel(
                 round_weight(nc.scalar.copy, name, pair)
 
         round_pass("w1p0")
-        gather_scales("left", left_list)
-        gather_scales("right", right_list)
         gather_words("left", left_list, 0)
         gather_words("right", right_list, 0)
+        gather_scales("left", left_list)
+        gather_scales("right", right_list)
         quantize_weight("w1p0", 0)
         quantize_weight("w1p0", 1)
         first_products("w1p0", "left", 0, True, False)
 
         round_pass("w2p0")
-        gather_words("left", left_list, 1)
-        gather_words("right", right_list, 1)
         quantize_weight("w2p0", 0)
         quantize_weight("w2p0", 1)
         first_products("w2p0", "right", 0, False, False)
 
+        gather_words("left", left_list, 1)
+        gather_words("right", right_list, 1)
         round_weight(nc.scalar.copy, "w1p1", 0)
-        round_weight(nc.vector.tensor_copy, "w1p1", 1)
+        round_weight(nc.vector.tensor_copy, "w1p1", 1, 0, 3 * P // 4)
+        round_weight(nc.scalar.copy, "w1p1", 1, 3 * P // 4, P)
         quantize_weight("w1p1", 0)
         quantize_weight("w1p1", 1)
         first_products("w1p1", "left", 1, False, False)
@@ -155,49 +157,57 @@ def tile_picked_yrecnn_relu_po_kernel(
         quantize_weight("w2p1", 1, 2)
         first_products("w2p1", "right", 1, False, True)
 
-        hidden = [keep.tile([P, S], F32, name=f"hidden{t}") for t in range(PACK)]
+        hidden = [keep.tile([P, S], F32, name=f"hidden{t}", align_bytes=64) for t in range(PACK)]
         nc.vector.tensor_scalar_max(hidden[0][:], h_banks[0][:], 0.0)
         for t in range(1, PACK):
             nc.scalar.activation(out=hidden[t][:], in_=h_banks[t][:], func=RELU)
 
         children, child_rounded, child_codes, child_scales = {}, {}, {}, {}
         for side in ("a", "ee"):
-            children[side] = keep.tile([P, PACK, V], F32, name=f"children_{side}")
-            child_rounded[side] = keep.tile([P, V, PACK], BF16, name=f"child_rounded_{side}", align_bytes=64)
-            child_codes[side] = keep.tile([P, V], U32, name=f"child_codes_{side}", align_bytes=64)
             child_scales[side] = keep.tile([P, V], U8, name=f"child_scales_{side}", align_bytes=64)
 
         def interleave(copy, dst, src):
             copy(
-                out=dst[:].rearrange("p (c i) t -> p c t i", i=4),
-                in_=src[:].rearrange("p t (c i) -> p c t i", i=4),
+                out=dst.rearrange("p (c i) t -> p c t i", i=4),
+                in_=src.rearrange("p t (c i) -> p c t i", i=4),
             )
 
         def quantize_tile(words, plane, values):
             nc.vector.quantize_mx(
-                out=words[:].bitcast(FP8X4), scales=plane[:], in_=values[:].rearrange("p v t -> p (v t)")
+                out=words.bitcast(FP8X4), scales=plane, in_=values[:].rearrange("p v t -> p (v t)")
             )
 
-        for t in range(PACK):
-            nc.vector.tensor_copy(out=children["a"][:, t, :], in_=hidden[t][:].indirect(up1_list[:]))
-            nc.vector.tensor_copy(out=children["ee"][:, t, :], in_=hidden[t][:].indirect(up2_list[:]))
+        def gather_children(side, picks, place):
+            children[side] = keep.tile([P, PACK, V], F32, name=place, align_bytes=64)
+            for t in range(PACK):
+                nc.vector.tensor_copy(out=children[side][:, t, :], in_=hidden[t][:].indirect(picks[:]))
+
+        gather_children("a", up1_list, "children_a")
+        child_rounded["a"] = keep.tile([P, V, PACK], BF16, name="child_rounded_a", align_bytes=64)
+        interleave(nc.vector.tensor_copy, child_rounded["a"][:], children["a"][:])
         round_pass("w3")
-        round_pass("w4")
-        interleave(nc.vector.tensor_copy, child_rounded["a"], children["a"])
-        interleave(nc.vector.tensor_copy, child_rounded["ee"], children["ee"])
         quantize_weight("w3", 0)
+        spare = psum.tile([P, S], F32, name="h_bank0")
+        for n in range(WARM_PASSES):
+            product(spare, "w3", 0, picked_words["left", 0][:], picked_scales["left"][:], True, True)
+        gather_children("ee", up2_list, "rounded_w3_0")
+        round_pass("w4")
+        child_rounded["ee"] = keep.tile([P, V, PACK], BF16, name="raw_w4", align_bytes=64)
+        interleave(nc.scalar.copy, child_rounded["ee"][:], children["ee"][:])
         quantize_weight("w3", 1)
-        quantize_tile(child_codes["a"], child_scales["a"], child_rounded["a"])
+        child_codes["a"] = keep.tile([P, V], U32, name="hidden3", align_bytes=64)
+        child_codes["ee"] = keep.tile([P, V], U32, name="child_codes_ee", align_bytes=64)
+        quantize_tile(child_codes["a"][:], child_scales["a"][:], child_rounded["a"])
         for t in range(PACK):
             product(y_banks[t], "w3", t, child_codes["a"][:], child_scales["a"][:], True, False)
-        quantize_tile(child_codes["ee"], child_scales["ee"], child_rounded["ee"])
         quantize_weight("w4", 0)
         quantize_weight("w4", 1)
+        quantize_tile(child_codes["ee"][:], child_scales["ee"][:], child_rounded["ee"])
         for t in range(PACK):
             product(y_banks[t], "w4", t, child_codes["ee"][:], child_scales["ee"][:], False, True)
 
         y = keep.tile([P, PACK, V], F32, name="y")
-        y_rounded = keep.tile([P, V, PACK], BF16, name="y_rounded", align_bytes=64)
+        y_rounded = [keep.tile([P, V // 2, PACK], BF16, name=f"y_rounded{half}", align_bytes=64) for half in range(2)]
         y_codes = keep.tile([P, V], I32, name="y_codes", align_bytes=64)
         y_scales = keep.tile([P, V], U8, name="y_scales", align_bytes=64)
         y_rows = out_0.rearrange("(p t) v -> p t v", t=PACK)
@@ -207,8 +217,11 @@ def tile_picked_yrecnn_relu_po_kernel(
             else:
                 nc.vector.tensor_scalar_max(y[:, t, :], y_banks[t][:], 0.0)
                 nc.sync.dma_start(out=y_rows[:, t - 1 : t + 1, :], in_=y[:, t - 1 : t + 1, :])
-        interleave(nc.vector.tensor_copy, y_rounded, y)
-        quantize_tile(y_codes, y_scales, y_rounded)
+        for half, copy in enumerate((nc.vector.tensor_copy, nc.scalar.copy)):
+            interleave(copy, y_rounded[half][:], y[:, :, half * V // 2 : (half + 1) * V // 2])
+        for half in range(2):
+            cols = slice(half * V // 2, (half + 1) * V // 2)
+            quantize_tile(y_codes[:, cols], y_scales[:, cols], y_rounded[half])
         nc.sync.dma_start(out=out_1[0].rearrange("p c r -> p (c r)").bitcast(I32), in_=y_codes[:])
         for q in range(4):
             queue = nc.scalar if q % 2 == 0 else nc.sync

@@ -26,6 +26,7 @@ def tile_picked_yrecnn_relu_po_kernel(
     nc = tc.nc
     with ExitStack() as ctx:
         keep = ctx.enter_context(tc.tile_pool(name="keep", bufs=1))
+        shared = ctx.enter_context(tc.tile_pool(name="shared", bufs=1))
         psum = ctx.enter_context(tc.psum_pool(name="psum", bufs=1))
 
         weights = {
@@ -37,7 +38,10 @@ def tile_picked_yrecnn_relu_po_kernel(
         for name in weights:
             raw[name] = keep.tile([P, PACK, K_PASS], F32, name=f"raw_{name}", align_bytes=64)
             for pair in range(2):
-                rounded[name, pair] = keep.tile([P, 2, P, PACK], BF16, name=f"rounded_{name}_{pair}", align_bytes=64)
+                if (name, pair) == ("w3", 0):
+                    rounded[name, pair] = shared.tile([P, 2, P, PACK], BF16, name="rounded_w3_0", align_bytes=64, offset=2048)
+                elif (name, pair) != ("w3", 1):
+                    rounded[name, pair] = keep.tile([P, 2, P, PACK], BF16, name=f"rounded_{name}_{pair}", align_bytes=64)
             codes[name] = keep.tile([P, K_PASS], U32, name=f"codes_{name}", align_bytes=64)
             scales[name] = keep.tile([P, K_PASS], U8, name=f"scales_{name}", align_bytes=64)
 
@@ -71,11 +75,7 @@ def tile_picked_yrecnn_relu_po_kernel(
         def load_words(o):
             nc.sync.dma_start(out=table_words[o][:], in_=x_words[o].rearrange("p c r -> p (c r)").bitcast(I32))
 
-        warm = keep.tile([P, 8], F32, name="warm")
-        warm_out = keep.tile([P, 8], F32, name="warm_out")
         nc.vector.memset(table_scales[:].bitcast(I32), 0)
-        nc.vector.memset(warm[:], 0.0)
-        nc.scalar.activation(out=warm_out[:], in_=warm[:], func=RELU)
 
         load_words(0)
         left_list = load_list(offs, "left_list")
@@ -124,9 +124,12 @@ def tile_picked_yrecnn_relu_po_kernel(
             for t in range(PACK):
                 product(h_banks[t], name, t, picked_words[side, o][:], picked_scales[side][4 * o : P, :], start, stop)
 
+        def round_on_scalar(out, in_):
+            nc.scalar.activation(out=out, in_=in_, func=mybir.ActivationFunctionType.Copy)
+
         def round_pass(name):
             for pair in range(2):
-                round_weight(nc.scalar.copy, name, pair)
+                round_weight(round_on_scalar, name, pair)
 
         round_pass("w1p0")
         gather_words("left", left_list, 0)
@@ -144,15 +147,16 @@ def tile_picked_yrecnn_relu_po_kernel(
 
         gather_words("left", left_list, 1)
         gather_words("right", right_list, 1)
-        round_weight(nc.scalar.copy, "w1p1", 0)
+        round_weight(round_on_scalar, "w1p1", 0)
         round_weight(nc.vector.tensor_copy, "w1p1", 1, 0, 3 * P // 4)
-        round_weight(nc.scalar.copy, "w1p1", 1, 3 * P // 4, P)
+        round_weight(round_on_scalar, "w1p1", 1, 3 * P // 4, P)
         quantize_weight("w1p1", 0)
         quantize_weight("w1p1", 1)
         first_products("w1p1", "left", 1, False, False)
 
         round_weight(nc.vector.tensor_copy, "w2p1", 0)
-        round_weight(nc.scalar.copy, "w2p1", 1)
+        round_weight(nc.vector.tensor_copy, "w2p1", 1, 0, P // 4)
+        round_weight(round_on_scalar, "w2p1", 1, P // 4, P)
         quantize_weight("w2p1", 0, 2)
         quantize_weight("w2p1", 1, 2)
         first_products("w2p1", "right", 1, False, True)
@@ -177,23 +181,30 @@ def tile_picked_yrecnn_relu_po_kernel(
                 out=words.bitcast(FP8X4), scales=plane, in_=values[:].rearrange("p v t -> p (v t)")
             )
 
-        def gather_children(side, picks, place):
-            children[side] = keep.tile([P, PACK, V], F32, name=place, align_bytes=64)
+        def gather_children(side, picks):
             for t in range(PACK):
                 nc.vector.tensor_copy(out=children[side][:, t, :], in_=hidden[t][:].indirect(picks[:]))
 
-        gather_children("a", up1_list, "children_a")
-        child_rounded["a"] = keep.tile([P, V, PACK], BF16, name="child_rounded_a", align_bytes=64)
-        interleave(nc.vector.tensor_copy, child_rounded["a"][:], children["a"][:])
-        round_pass("w3")
+        def round_on_gpsimd(out, in_):
+            nc.gpsimd.tensor_scalar(out, in_, 1.0, 0.0, op0=mybir.AluOpType.mult, op1=mybir.AluOpType.add)
+
+        children["a"] = keep.tile([P, PACK, V], F32, name="children_a")
+        gather_children("a", up1_list)
+        round_weight(round_on_scalar, "w3", 0)
+        rounded["w3", 1] = keep.tile([P, 2, P, PACK], BF16, name="rounded_w2p1_1", align_bytes=64)
+        round_on_gpsimd(rounded["w3", 1][:], raw["w3"][:].rearrange("p j (m u e) -> p u e m j", u=2, e=2)[:, 1])
         quantize_weight("w3", 0)
+        child_rounded["a"] = shared.tile([P, V, PACK], BF16, name="child_rounded_a", align_bytes=64, offset=1024)
+        round_on_gpsimd(child_rounded["a"][:], children["a"][:].rearrange("p t v -> p v t"))
+        children["ee"] = shared.tile([P, PACK, V], F32, name="children_ee", align_bytes=64, offset=3072)
         spare = psum.tile([P, S], F32, name="h_bank0")
         for n in range(WARM_PASSES):
             product(spare, "w3", 0, picked_words["left", 0][:], picked_scales["left"][:], True, True)
-        gather_children("ee", up2_list, "rounded_w3_0")
+        gather_children("ee", up2_list)
         round_pass("w4")
         child_rounded["ee"] = keep.tile([P, V, PACK], BF16, name="raw_w4", align_bytes=64)
-        interleave(nc.scalar.copy, child_rounded["ee"][:], children["ee"][:])
+        interleave(nc.vector.tensor_copy, child_rounded["ee"][:, 0 : V // 4, :], children["ee"][:, :, 0 : V // 4])
+        interleave(nc.scalar.copy, child_rounded["ee"][:, V // 4 : V, :], children["ee"][:, :, V // 4 : V])
         quantize_weight("w3", 1)
         child_codes["a"] = keep.tile([P, V], U32, name="hidden3", align_bytes=64)
         child_codes["ee"] = keep.tile([P, V], U32, name="child_codes_ee", align_bytes=64)

from contextlib import ExitStack

import concourse.mybir as mybir

K, T, S, V, H, N = 1024, 1024, 512, 256, 512, 512
FLOPS = 2 * (2 * K * H * S + 2 * H * N * V)

F32 = mybir.dt.float32
BF16 = mybir.dt.bfloat16
I32 = mybir.dt.int32
U32 = mybir.dt.uint32
U16 = mybir.dt.uint16
U8 = mybir.dt.uint8
FP8X4 = mybir.dt.float8_e4m3fn_x4
RELU = mybir.ActivationFunctionType.Relu

P = 128
PACK = 4
K_PASS = P * PACK
WARM_PASSES = 4


def tile_picked_yrecnn_relu_po_kernel(
    tc, x_words, x_scales, w1, w2, w3, w4, offs, right, up1, up2, out_0, out_1, out_2
):
    nc = tc.nc
    with ExitStack() as ctx:
        keep = ctx.enter_context(tc.tile_pool(name="keep", bufs=1))
        shared = ctx.enter_context(tc.tile_pool(name="shared", bufs=1))
        psum = ctx.enter_context(tc.psum_pool(name="psum", bufs=1))

        weights = {
            "w1p0": w1[0:K_PASS, :], "w1p1": w1[K_PASS:K, :],
            "w2p0": w2[0:K_PASS, :], "w2p1": w2[K_PASS:K, :],
            "w3": w3, "w4": w4,
        }
        raw, rounded, codes, scales = {}, {}, {}, {}
        for name in weights:
            raw[name] = keep.tile([P, PACK, K_PASS], F32, name=f"raw_{name}", align_bytes=64)
            for pair in range(2):
                if (name, pair) == ("w3", 0):
                    rounded[name, pair] = shared.tile([P, 2, P, PACK], BF16, name="rounded_w3_0", align_bytes=64, offset=2048)
                elif (name, pair) != ("w3", 1):
                    rounded[name, pair] = keep.tile([P, 2, P, PACK], BF16, name=f"rounded_{name}_{pair}", align_bytes=64)
            codes[name] = keep.tile([P, K_PASS], U32, name=f"codes_{name}", align_bytes=64)
            scales[name] = keep.tile([P, K_PASS], U8, name=f"scales_{name}", align_bytes=64)

        def load_weight(name):
            nc.sync.dma_start(out=raw[name][:], in_=weights[name].rearrange("(p j) c -> p j c", j=PACK))

        def load_list(source, name):
            tile = keep.tile(list(source.shape), U16, name=name)
            nc.sync.dma_start(out=tile[:], in_=source)
            return tile

        def round_weight(copy, name, pair, start=0, stop=P):
            src = raw[name][:].rearrange("p j (m u e) -> p u m j e", u=2, e=2)[:, pair, start:stop]
            dst = rounded[name, pair][:, :, start:stop, :].rearrange("p e m j -> p m j e")
            copy(out=dst, in_=src)

        def quantize_weight(name, pair, pieces=1):
            flat = rounded[name, pair][:].rearrange("p e m j -> p (e m j)")
            width = 2 * P // pieces
            for piece in range(pieces):
                cols = slice(pair * 2 * P + piece * width, pair * 2 * P + (piece + 1) * width)
                nc.vector.quantize_mx(
                    out=codes[name][:, cols].bitcast(FP8X4),
                    scales=scales[name][:, cols],
                    in_=flat[:, piece * width * PACK : (piece + 1) * width * PACK],
                )

        table_words = [keep.tile([P, T], I32, name=f"table_words{o}") for o in range(2)]
        table_scales = keep.tile([P, T], U8, name="table_scales")

        def load_words(o):
            nc.sync.dma_start(out=table_words[o][:], in_=x_words[o].rearrange("p c r -> p (c r)").bitcast(I32))

        nc.vector.memset(table_scales[:].bitcast(I32), 0)

        load_words(0)
        left_list = load_list(offs, "left_list")
        right_list = load_list(right, "right_list")
        for q in range(4):
            nc.sync.dma_start(
                out=table_scales[32 * q : 32 * q + 8, :].bitcast(I32),
                in_=x_scales[:, 4 * q : 4 * q + 4, :].bitcast(I32),
            )
        load_weight("w1p0")
        load_weight("w2p0")
        load_words(1)
        load_weight("w1p1")
        load_weight("w2p1")
        up1_list = load_list(up1, "up1_list")
        up2_list = load_list(up2, "up2_list")
        load_weight("w3")
        load_weight("w4")

        picked_words, picked_scales = {}, {}

        def gather_words(side, picks, o):
            picked_words[side, o] = keep.tile([P, S], U32, name=f"picked_words_{side}{o}", align_bytes=64)
            nc.vector.tensor_copy(out=picked_words[side, o][:], in_=table_words[o][:].bitcast(U32).indirect(picks[:]))

        def gather_scales(side, picks):
            picked_scales[side] = keep.tile([P, S], U8, name=f"picked_scales_{side}", align_bytes=64)
            nc.vector.tensor_copy(out=picked_scales[side][:], in_=table_scales[:].indirect(picks[:]))

        h_banks = [psum.tile([P, S], F32, name=f"h_bank{t}") for t in range(PACK)]
        y_banks = [psum.tile([P, V], F32, name=f"y_bank{t}") for t in range(PACK)]

        def product(bank, name, t, words, plane, start, stop):
            cols = slice(t * P, (t + 1) * P)
            nc.tensor.matmul_mx(
                out=bank[:],
                lhsT=codes[name][:, cols].bitcast(FP8X4),
                lhsT_scale=scales[name][:, cols],
                rhs=words.bitcast(FP8X4),
                rhs_scale=plane,
                start=start,
                stop=stop,
            )

        def first_products(name, side, o, start, stop):
            for t in range(PACK):
                product(h_banks[t], name, t, picked_words[side, o][:], picked_scales[side][4 * o : P, :], start, stop)

        def round_on_scalar(out, in_):
            nc.scalar.activation(out=out, in_=in_, func=mybir.ActivationFunctionType.Copy)

        def round_pass(name):
            for pair in range(2):
                round_weight(round_on_scalar, name, pair)

        round_pass("w1p0")
        gather_words("left", left_list, 0)
        gather_words("right", right_list, 0)
        gather_scales("left", left_list)
        gather_scales("right", right_list)
        quantize_weight("w1p0", 0)
        quantize_weight("w1p0", 1)
        first_products("w1p0", "left", 0, True, False)

        round_pass("w2p0")
        quantize_weight("w2p0", 0)
        quantize_weight("w2p0", 1)
        first_products("w2p0", "right", 0, False, False)

        gather_words("left", left_list, 1)
        gather_words("right", right_list, 1)
        round_weight(round_on_scalar, "w1p1", 0)
        round_weight(nc.vector.tensor_copy, "w1p1", 1, 0, 3 * P // 4)
        round_weight(round_on_scalar, "w1p1", 1, 3 * P // 4, P)
        quantize_weight("w1p1", 0)
        quantize_weight("w1p1", 1)
        first_products("w1p1", "left", 1, False, False)

        round_weight(nc.vector.tensor_copy, "w2p1", 0)
        round_weight(nc.vector.tensor_copy, "w2p1", 1, 0, P // 4)
        round_weight(round_on_scalar, "w2p1", 1, P // 4, P)
        quantize_weight("w2p1", 0, 2)
        quantize_weight("w2p1", 1, 2)
        first_products("w2p1", "right", 1, False, True)

        hidden = [keep.tile([P, S], F32, name=f"hidden{t}", align_bytes=64) for t in range(PACK)]
        nc.vector.tensor_scalar_max(hidden[0][:], h_banks[0][:], 0.0)
        for t in range(1, PACK):
            nc.scalar.activation(out=hidden[t][:], in_=h_banks[t][:], func=RELU)

        children, child_rounded, child_codes, child_scales = {}, {}, {}, {}
        for side in ("a", "ee"):
            child_scales[side] = keep.tile([P, V], U8, name=f"child_scales_{side}", align_bytes=64)

        def interleave(copy, dst, src):
            copy(
                out=dst.rearrange("p (c i) t -> p c t i", i=4),
                in_=src.rearrange("p t (c i) -> p c t i", i=4),
            )

        def quantize_tile(words, plane, values):
            nc.vector.quantize_mx(
                out=words.bitcast(FP8X4), scales=plane, in_=values[:].rearrange("p v t -> p (v t)")
            )

        def gather_children(side, picks):
            for t in range(PACK):
                nc.vector.tensor_copy(out=children[side][:, t, :], in_=hidden[t][:].indirect(picks[:]))

        def round_on_gpsimd(out, in_):
            nc.gpsimd.tensor_scalar(out, in_, 1.0, 0.0, op0=mybir.AluOpType.mult, op1=mybir.AluOpType.add)

        children["a"] = keep.tile([P, PACK, V], F32, name="children_a")
        gather_children("a", up1_list)
        round_weight(round_on_scalar, "w3", 0)
        rounded["w3", 1] = keep.tile([P, 2, P, PACK], BF16, name="rounded_w2p1_1", align_bytes=64)
        round_on_gpsimd(rounded["w3", 1][:], raw["w3"][:].rearrange("p j (m u e) -> p u e m j", u=2, e=2)[:, 1])
        quantize_weight("w3", 0)
        child_rounded["a"] = shared.tile([P, V, PACK], BF16, name="child_rounded_a", align_bytes=64, offset=1024)
        round_on_gpsimd(child_rounded["a"][:], children["a"][:].rearrange("p t v -> p v t"))
        children["ee"] = shared.tile([P, PACK, V], F32, name="children_ee", align_bytes=64, offset=3072)
        spare = psum.tile([P, S], F32, name="h_bank0")
        for n in range(WARM_PASSES):
            product(spare, "w3", 0, picked_words["left", 0][:], picked_scales["left"][:], True, True)
        gather_children("ee", up2_list)
        round_pass("w4")
        child_rounded["ee"] = keep.tile([P, V, PACK], BF16, name="raw_w4", align_bytes=64)
        interleave(nc.vector.tensor_copy, child_rounded["ee"][:, 0 : V // 4, :], children["ee"][:, :, 0 : V // 4])
        interleave(nc.scalar.copy, child_rounded["ee"][:, V // 4 : V, :], children["ee"][:, :, V // 4 : V])
        quantize_weight("w3", 1)
        child_codes["a"] = keep.tile([P, V], U32, name="hidden3", align_bytes=64)
        child_codes["ee"] = keep.tile([P, V], U32, name="child_codes_ee", align_bytes=64)
        quantize_tile(child_codes["a"][:], child_scales["a"][:], child_rounded["a"])
        for t in range(PACK):
            product(y_banks[t], "w3", t, child_codes["a"][:], child_scales["a"][:], True, False)
        quantize_weight("w4", 0)
        quantize_weight("w4", 1)
        quantize_tile(child_codes["ee"][:], child_scales["ee"][:], child_rounded["ee"])
        for t in range(PACK):
            product(y_banks[t], "w4", t, child_codes["ee"][:], child_scales["ee"][:], False, True)

        y = keep.tile([P, PACK, V], F32, name="y")
        y_rounded = [keep.tile([P, V // 2, PACK], BF16, name=f"y_rounded{half}", align_bytes=64) for half in range(2)]
        y_codes = keep.tile([P, V], I32, name="y_codes", align_bytes=64)
        y_scales = keep.tile([P, V], U8, name="y_scales", align_bytes=64)
        y_rows = out_0.rearrange("(p t) v -> p t v", t=PACK)
        for t in range(PACK):
            if t % 2 == 0:
                nc.scalar.activation(out=y[:, t, :], in_=y_banks[t][:], func=RELU)
            else:
                nc.vector.tensor_scalar_max(y[:, t, :], y_banks[t][:], 0.0)
                nc.sync.dma_start(out=y_rows[:, t - 1 : t + 1, :], in_=y[:, t - 1 : t + 1, :])
        for half, copy in enumerate((nc.vector.tensor_copy, nc.scalar.copy)):
            interleave(copy, y_rounded[half][:], y[:, :, half * V // 2 : (half + 1) * V // 2])
        for half in range(2):
            cols = slice(half * V // 2, (half + 1) * V // 2)
            quantize_tile(y_codes[:, cols], y_scales[:, cols], y_rounded[half])
        nc.sync.dma_start(out=out_1[0].rearrange("p c r -> p (c r)").bitcast(I32), in_=y_codes[:])
        for q in range(4):
            queue = nc.scalar if q % 2 == 0 else nc.sync
            queue.dma_start(
                out=out_2[0, 4 * q : 4 * q + 4, :].bitcast(I32),
                in_=y_scales[32 * q : 32 * q + 4, :].bitcast(I32),
            )
